import numpy as np
import ml_dtypes


def mxq(x, axis, fmt="e4m3"):
    dtype, down = {"e4m3": (ml_dtypes.float8_e4m3fn, 7), "e5m2": (ml_dtypes.float8_e5m2, 14)}[fmt]
    v = np.moveaxis(np.asarray(x, np.float32).astype(ml_dtypes.bfloat16).astype(np.float64), axis, -1)
    blocks = v.reshape(v.shape[:-1] + (-1, 32))
    amax = np.abs(blocks).max(-1, keepdims=True)
    byte = np.maximum(np.where(amax > 0, np.frexp(amax)[1] - 1 + 127, 0) - down, 1)
    scale = np.exp2(byte - 127.0)
    codes = (blocks / scale).astype(np.float32).astype(dtype).astype(np.float64)
    return np.moveaxis((codes * scale).reshape(v.shape), -1, axis)


WIDE = False


def mx_kscale(k):
    if not WIDE:
        return np.ones(k)
    levels = np.array([10, -10, 5, -5, 0])
    if k % 512:
        return np.exp2(np.random.permutation(np.resize(levels, k // 32))).repeat(32)
    a = np.empty((k // 512, 16))
    for p in range(k // 512):
        a[p, :8] = np.random.permutation(np.resize(levels, 8))
        for g in range(8):
            far = levels[np.abs(levels - a[p, g]) >= 10]
            a[p, g + 8] = far[np.random.randint(len(far))]
    return np.exp2(a.ravel()).repeat(32)


def f64(x):
    return np.asarray(x).astype(np.float64)


def striped8(idx):
    return np.asarray(idx).reshape(8, -1, 16).transpose(0, 2, 1).reshape(128, -1).astype(np.uint16)


def unstriped8(offs):
    return offs.reshape(8, 16, -1).transpose(0, 2, 1).reshape(8, -1).astype(np.int64)


def pick8(x, idx, run):
    r = np.arange(len(x))
    return x[r[:, None], idx[r % (8 * run) // run]]


E2M1 = np.array([0.0, 0.5, 1.0, 1.5, 2.0, 3.0, 4.0, 6.0, -0.0, -0.5, -1.0, -1.5, -2.0, -3.0, -4.0, -6.0])


def pack_weight(w, fmt):
    k, n = w.shape
    w = f64(np.asarray(w, np.float32).astype(ml_dtypes.bfloat16)).reshape(k // 32, 32, n)
    amax = np.abs(w).max(1)
    if fmt == "e4m3":
        byte = np.frexp(amax)[1] - 1 + 127 - 7
    else:
        mant, ex = np.frexp(amax / 6.0)
        byte = np.where(mant > 0.5, ex, ex - 1) + 127
    byte = np.clip(np.where(amax > 0, byte, 1), 1, 254)
    scaled = (w * np.exp2(127.0 - byte)[:, None, :]).reshape(k, n).astype(np.float32)
    by_word = np.ascontiguousarray(scaled.reshape(k // 512, 128, 4, n).transpose(0, 1, 3, 2))
    if fmt == "e4m3":
        words = by_word.astype(ml_dtypes.float8_e4m3fn).view(np.uint8)
    else:
        c = by_word.astype(ml_dtypes.float4_e2m1fn).view(np.uint8) & 0xF
        words = (c[..., 0::2] | (c[..., 1::2] << 4)).reshape(k // 512, 128, 2 * n)
    return np.ascontiguousarray(words), np.ascontiguousarray(byte.astype(np.uint8).reshape(k // 512, 16, n))


def unpack_weight(words, scales, fmt):
    g, _, n = scales.shape
    words = np.ascontiguousarray(words).reshape(g, 128, n, -1)
    if fmt == "e4m3":
        vals = words.view(ml_dtypes.float8_e4m3fn).astype(np.float64)
    else:
        nib = np.empty((g, 128, n, 4), np.uint8)
        nib[..., 0::2] = words & 0xF
        nib[..., 1::2] = words >> 4
        vals = E2M1[nib]
    vals = vals * np.repeat(np.exp2(scales.astype(np.float64) - 127.0), 8, axis=1)[..., None]
    return vals.transpose(0, 1, 3, 2).reshape(g * 512, n)


D, K, T, U, X, S, I, Q = 512, 512, 1024, 1024, 1024, 1024, 512, 128


def setup_inputs():
    n = np.random.standard_normal
    idx = np.stack([np.random.permutation(T)[:I] for _ in range(8)])
    idx2 = np.stack([np.random.permutation(U)[:I] for _ in range(8)])
    idx3 = np.stack([np.random.permutation(U)[:I] for _ in range(8)])
    idx4 = np.stack([np.random.permutation(X)[:I] for _ in range(8)])
    idx5 = np.stack([np.random.permutation(X)[:I] for _ in range(8)])
    idx6 = np.stack([np.random.permutation(S)[:I] for _ in range(8)])
    idx7 = np.stack([np.random.permutation(S)[:I] for _ in range(8)])
    fd = mx_kscale(D)
    fk = mx_kscale(K)
    wqp = pack_weight(n((D, K)) * 1.0 / np.sqrt(D) * fd[:, None] * fk, "e4m3")
    keysp = pack_weight(n((K, T)) * 1.0 / np.sqrt(K) / fk[:, None], "e4m3")
    notesp = pack_weight(n((K, U)) * 1.0 / np.sqrt(K) / fk[:, None], "e2m1")
    usersp = pack_weight(n((D, X)) * 1.0 / np.sqrt(D) * fd[:, None], "e4m3")
    shelvesp = pack_weight(n((D, S)) * 1.0 / np.sqrt(D) * fd[:, None], "e2m1")
    return {
        "states": (n((D, Q)) * 0.95 / fd[:, None]).astype(np.float32),
        "wq_words": wqp[0],
        "wq_scales": wqp[1],
        "keys_words": keysp[0],
        "keys_scales": keysp[1],
        "notes_words": notesp[0],
        "notes_scales": notesp[1],
        "users_words": usersp[0],
        "users_scales": usersp[1],
        "shelves_words": shelvesp[0],
        "shelves_scales": shelvesp[1],
        "offs": striped8(idx),
        "offs2": striped8(idx2),
        "offs3": striped8(idx3),
        "offs4": striped8(idx4),
        "offs5": striped8(idx5),
        "offs6": striped8(idx6),
        "offs7": striped8(idx7),
    }


def reference(states, wq_words, wq_scales, keys_words, keys_scales, notes_words, notes_scales, users_words, users_scales, shelves_words, shelves_scales, offs, offs2, offs3, offs4, offs5, offs6, offs7):
    idx = unstriped8(offs)
    idx2 = unstriped8(offs2)
    idx3 = unstriped8(offs3)
    idx4 = unstriped8(offs4)
    idx5 = unstriped8(offs5)
    idx6 = unstriped8(offs6)
    idx7 = unstriped8(offs7)
    wqu = unpack_weight(wq_words, wq_scales, "e4m3")
    keysu = unpack_weight(keys_words, keys_scales, "e4m3")
    notesu = unpack_weight(notes_words, notes_scales, "e2m1")
    usersu = unpack_weight(users_words, users_scales, "e4m3")
    shelvesu = unpack_weight(shelves_words, shelves_scales, "e2m1")
    statesq = mxq(f64(states), 0, "e4m3")
    qv = wqu.T @ statesq
    qvq = mxq(qv, 0, "e4m3")
    a = qvq.T @ keysu
    b = qvq.T @ notesu
    c0 = statesq.T @ usersu
    d0 = statesq.T @ shelvesu
    f1 = np.zeros((Q, U))
    f1[np.arange(Q)[:, None], idx2[np.arange(Q) % 128 // 16]] = pick8(a, idx, 16)
    bb = b + f1
    f2 = np.zeros((Q, X))
    f2[np.arange(Q)[:, None], idx4[np.arange(Q) % 128 // 16]] = pick8(bb, idx3, 16)
    cc = c0 - f2
    f3 = np.zeros((Q, S))
    f3[np.arange(Q)[:, None], idx6[np.arange(Q) % 128 // 16]] = pick8(cc, idx5, 16)
    dd = d0 + f3
    y = pick8(dd, idx7, 16)
    return y

@@ -1,0 +1,183 @@
+from contextlib import ExitStack
+
+import concourse.mybir as mybir
+
+F32 = mybir.dt.float32
+BF16 = mybir.dt.bfloat16
+I32 = mybir.dt.int32
+U32 = mybir.dt.uint32
+U16 = mybir.dt.uint16
+U8 = mybir.dt.uint8
+FP8X4 = mybir.dt.float8_e4m3fn_x4
+FP4X4 = mybir.dt.float4_e2m1fn_x4
+ADD = mybir.AluOpType.add
+SUBTRACT = mybir.AluOpType.subtract
+COPY = mybir.ActivationFunctionType.Copy
+
+P = 128
+PACK = 4
+D, K, COLS, SLOTS, Q = 512, 512, 1024, 512, 128
+BANK = 512
+A_PIECE = 256
+CAST_SPLIT = 96
+HALF = SLOTS // 2
+HALF_COLS = HALF // 16
+
+FLOPS = 2 * D * K * Q + 4 * 2 * K * Q * COLS
+
+
+def tile_attend_relayfour_madefour_kernel(
+    tc, states, wq_words, wq_scales, keys_words, keys_scales, notes_words, notes_scales,
+    users_words, users_scales, shelves_words, shelves_scales,
+    offs, offs2, offs3, offs4, offs5, offs6, offs7, out,
+):
+    nc = tc.nc
+    with ExitStack() as ctx:
+        lists = ctx.enter_context(tc.tile_pool(name="lists", bufs=1))
+        sb = ctx.enter_context(tc.tile_pool(name="sb", bufs=1))
+        psum = ctx.enter_context(tc.psum_pool(name="psum", bufs=1))
+
+        def zeroed_scales(name, width):
+            tile = sb.tile([P, width], U8, name=name, align_bytes=64)
+            nc.vector.memset(tile[:].bitcast(U32), 0)
+            return tile
+
+        def load_scales(queue, tile, rows):
+            for quad in range(4):
+                queue.dma_start(
+                    out=tile[32 * quad : 32 * quad + 4, :].bitcast(I32),
+                    in_=rows[0, 4 * quad : 4 * quad + 4, :].bitcast(I32),
+                )
+
+        def load_fp8(name, words, width):
+            tile = sb.tile([P, width], U32, name=name, align_bytes=64)
+            nc.sync.dma_start(out=tile[:].bitcast(I32), in_=words[0].rearrange("p n t -> p (n t)").bitcast(I32))
+            return tile
+
+        def load_fp4(name, words):
+            tile = sb.tile([P, 2 * COLS], U8, name=name, align_bytes=64)
+            nc.sync.dma_start(out=tile[:].bitcast(I32), in_=words[0].bitcast(I32))
+            return tile
+
+        def load_list(name, src):
+            tile = lists.tile([P, SLOTS // 16], U16, name=name)
+            nc.sync.dma_start(tile[:], src)
+            return tile
+
+        wq_s = zeroed_scales("wq_s", K)
+        keys_s = zeroed_scales("keys_s", COLS)
+        notes_s = zeroed_scales("notes_s", COLS)
+        users_s = zeroed_scales("users_s", COLS)
+        shelves_s = zeroed_scales("shelves_s", COLS)
+        placed = []
+        for stage in range(3):
+            tile = sb.tile([P, COLS], F32, name="placed%d" % stage)
+            nc.gpsimd.memset(tile[:], 0.0)
+            placed.append(tile)
+
+        states_raw = sb.tile([P, PACK, Q], F32, name="states_raw")
+        nc.sync.dma_start(out=states_raw[:], in_=states.rearrange("(p j) q -> p j q", j=PACK))
+        load_scales(nc.scalar, wq_s, wq_scales)
+        wq_w = load_fp8("wq_w", wq_words, K)
+        keys_w = load_fp8("keys_w", keys_words, COLS)
+        load_scales(nc.sync, keys_s, keys_scales)
+        l1 = load_list("l1", offs)
+        l2 = load_list("l2", offs2)
+        notes_w = load_fp4("notes_w", notes_words)
+        load_scales(nc.sync, notes_s, notes_scales)
+        l3 = load_list("l3", offs3)
+        l4 = load_list("l4", offs4)
+        users_w = load_fp8("users_w", users_words, COLS)
+        load_scales(nc.sync, users_s, users_scales)
+        l5 = load_list("l5", offs5)
+        l6 = load_list("l6", offs6)
+        shelves_w = load_fp4("shelves_w", shelves_words)
+        load_scales(nc.sync, shelves_s, shelves_scales)
+        l7 = load_list("l7", offs7)
+
+        wq_s_dealt = sb.tile([P, PACK, P], U8, name="wq_s_dealt", align_bytes=64)
+        nc.vector.tensor_copy(
+            out=wq_s_dealt[:].rearrange("p t m -> p m t"),
+            in_=wq_s[:].rearrange("p (m t) -> p m t", t=PACK),
+        )
+
+        states_bf = sb.tile([P, Q, PACK], BF16, name="states_bf", align_bytes=64)
+        states_by_q = states_raw[:].rearrange("p j q -> p q j")
+        nc.vector.tensor_copy(out=states_bf[:, :CAST_SPLIT, :], in_=states_by_q[:, :CAST_SPLIT, :])
+        nc.scalar.activation(states_bf[:, CAST_SPLIT:, :], states_by_q[:, CAST_SPLIT:, :], COPY)
+        states_c = sb.tile([P, Q], U32, name="states_c", align_bytes=64)
+        states_s = sb.tile([P, Q], U8, name="states_s", align_bytes=64)
+        nc.vector.quantize_mx(
+            out=states_c[:].bitcast(FP8X4), scales=states_s[:], in_=states_bf[:].rearrange("p q j -> p (q j)")
+        )
+
+        wq_w_dealt = sb.tile([P, PACK, P], U32, name="wq_w_dealt", align_bytes=64)
+        nc.scalar.copy(
+            out=wq_w_dealt[:].rearrange("p t m -> p m t"),
+            in_=wq_w[:].rearrange("p (m t) -> p m t", t=PACK),
+        )
+
+        qv = psum.tile([P, PACK, Q], F32, name="qv", tag="bank_qv")
+        for t in range(PACK):
+            nc.tensor.matmul_mx(
+                out=qv[:, t, :], lhsT=wq_w_dealt[:, t, :].bitcast(FP8X4), lhsT_scale=wq_s_dealt[:, t, :],
+                rhs=states_c[:].bitcast(FP8X4), rhs_scale=states_s[:], start=True, stop=True,
+            )
+        qv_bf = sb.tile([P, Q, PACK], BF16, name="qv_bf", align_bytes=64)
+        nc.scalar.copy(out=qv_bf[:], in_=qv[:].rearrange("p t q -> p q t"))
+        qv_c = sb.tile([P, Q], U32, name="qv_c", align_bytes=64)
+        qv_s = sb.tile([P, Q], U8, name="qv_s", align_bytes=64)
+        nc.vector.quantize_mx(
+            out=qv_c[:].bitcast(FP8X4), scales=qv_s[:], in_=qv_bf[:].rearrange("p q t -> p (q t)")
+        )
+
+        def scores(name, tag, codes, scales, moving, moving_scales):
+            bank = psum.tile([P, moving_scales.shape[1]], F32, name=name, tag=tag)
+            nc.tensor.matmul_mx(
+                out=bank[:], lhsT=codes[:].bitcast(FP8X4), lhsT_scale=scales[:],
+                rhs=moving, rhs_scale=moving_scales, start=True, stop=True,
+            )
+            return bank
+
+        def fp8_cols(words, c0, c1):
+            return words[:, c0:c1].bitcast(FP8X4)
+
+        def fp4_cols(words, c0, c1):
+            return words[:, 2 * c0 : 2 * c1].bitcast(FP4X4)
+
+        a = sb.tile([P, COLS], F32, name="a")
+        for piece in range(COLS // A_PIECE):
+            c0, c1 = piece * A_PIECE, (piece + 1) * A_PIECE
+            bank = scores("a%d" % piece, "bank%d" % piece, qv_c, qv_s, fp8_cols(keys_w, c0, c1), keys_s[:, c0:c1])
+            if piece % 2 == 0:
+                nc.scalar.copy(out=a[:, c0:c1], in_=bank[:])
+            else:
+                nc.vector.tensor_copy(out=a[:, c0:c1], in_=bank[:])
+
+        halves = [(h * BANK, (h + 1) * BANK) for h in range(COLS // BANK)]
+        b = [scores("b%d" % h, "bank%d" % (4 + h), qv_c, qv_s, fp4_cols(notes_w, c0, c1), notes_s[:, c0:c1])
+             for h, (c0, c1) in enumerate(halves)]
+        c = [scores("c%d" % h, "bank%d" % h, states_c, states_s, fp8_cols(users_w, c0, c1), users_s[:, c0:c1])
+             for h, (c0, c1) in enumerate(halves)]
+        d = [scores("d%d" % h, "bank%d" % (2 + h), states_c, states_s, fp4_cols(shelves_w, c0, c1), shelves_s[:, c0:c1])
+             for h, (c0, c1) in enumerate(halves)]
+
+        def gather(window, offsets, first, second):
+            nc.vector.tensor_copy(first, window[:].indirect(offsets[:, :HALF_COLS]))
+            nc.scalar.activation(second, window[:].indirect(offsets[:, HALF_COLS:]), COPY)
+
+        window = a
+        stages = ((l1, l2, b, ADD), (l3, l4, c, SUBTRACT), (l5, l6, d, ADD))
+        for stage, (pick, put, banks, op) in enumerate(stages):
+            picked = sb.tile([P, SLOTS], F32, name="picked%d" % stage)
+            gather(window, pick, picked[:, :HALF], picked[:, HALF:])
+            nc.vector.tensor_copy(placed[stage][:].indirect(put[:]), picked[:])
+            window = sb.tile([P, COLS], F32, name="sum%d" % stage)
+            for bank, (c0, c1) in zip(banks, halves):
+                nc.vector.tensor_tensor(window[:, c0:c1], bank[:], placed[stage][:, c0:c1], op)
+
+        y0 = sb.tile([P, HALF], F32, name="y0")
+        y1 = sb.tile([P, HALF], F32, name="y1")
+        gather(window, l7, y0[:], y1[:])
+        nc.sync.dma_start(out=out[:, :HALF], in_=y0[:])
+        nc.scalar.dma_start(out=out[:, HALF:], in_=y1[:])

@@ -37,9 +37,9 @@ def tile_attend_relayfour_madefour_kernel(
         sb = ctx.enter_context(tc.tile_pool(name="sb", bufs=1))
         psum = ctx.enter_context(tc.psum_pool(name="psum", bufs=1))
 
-        def zeroed_scales(name, width):
+        def zeroed_scales(engine, name, width):
             tile = sb.tile([P, width], U8, name=name, align_bytes=64)
-            nc.vector.memset(tile[:].bitcast(U32), 0)
+            engine.memset(tile[:].bitcast(U32), 0)
             return tile
 
         def load_scales(queue, tile, rows):
@@ -64,25 +64,27 @@ def tile_attend_relayfour_madefour_kernel(
             nc.sync.dma_start(tile[:], src)
             return tile
 
-        wq_s = zeroed_scales("wq_s", K)
-        keys_s = zeroed_scales("keys_s", COLS)
-        notes_s = zeroed_scales("notes_s", COLS)
-        users_s = zeroed_scales("users_s", COLS)
-        shelves_s = zeroed_scales("shelves_s", COLS)
-        placed = []
-        for stage in range(3):
-            tile = sb.tile([P, COLS], F32, name="placed%d" % stage)
-            nc.gpsimd.memset(tile[:], 0.0)
-            placed.append(tile)
+        wq_s = zeroed_scales(nc.vector, "wq_s", K)
+        keys_s = zeroed_scales(nc.vector, "keys_s", COLS)
+        notes_s = zeroed_scales(nc.gpsimd, "notes_s", COLS)
+        users_s = zeroed_scales(nc.gpsimd, "users_s", COLS)
+        shelves_s = zeroed_scales(nc.gpsimd, "shelves_s", COLS)
+
+        def zeroed_window(name, tag):
+            tile = sb.tile([P, COLS], F32, name=name, tag=tag, align_bytes=64)
+            nc.vector.memset(tile[:], 0.0)
+            return tile
+
+        placed = [zeroed_window("placed0", "placed0")]
 
         states_raw = sb.tile([P, PACK, Q], F32, name="states_raw")
         nc.sync.dma_start(out=states_raw[:], in_=states.rearrange("(p j) q -> p j q", j=PACK))
-        load_scales(nc.scalar, wq_s, wq_scales)
+        load_scales(nc.sync, wq_s, wq_scales)
         wq_w = load_fp8("wq_w", wq_words, K)
-        keys_w = load_fp8("keys_w", keys_words, COLS)
-        load_scales(nc.sync, keys_s, keys_scales)
         l1 = load_list("l1", offs)
         l2 = load_list("l2", offs2)
+        keys_w = load_fp8("keys_w", keys_words, COLS)
+        load_scales(nc.sync, keys_s, keys_scales)
         notes_w = load_fp4("notes_w", notes_words)
         load_scales(nc.sync, notes_s, notes_scales)
         l3 = load_list("l3", offs3)
@@ -96,12 +98,13 @@ def tile_attend_relayfour_madefour_kernel(
         l7 = load_list("l7", offs7)
 
         wq_s_dealt = sb.tile([P, PACK, P], U8, name="wq_s_dealt", align_bytes=64)
-        nc.vector.tensor_copy(
-            out=wq_s_dealt[:].rearrange("p t m -> p m t"),
-            in_=wq_s[:].rearrange("p (m t) -> p m t", t=PACK),
-        )
+        for t in (0, 2):
+            nc.vector.tensor_copy(
+                out=wq_s_dealt[:, t : t + 2, :].rearrange("p t m -> p m t"),
+                in_=wq_s[:].rearrange("p (m t) -> p m t", t=PACK)[:, :, t : t + 2],
+            )
 
-        states_bf = sb.tile([P, Q, PACK], BF16, name="states_bf", align_bytes=64)
+        states_bf = sb.tile([P, Q, PACK], BF16, name="states_bf", tag="states_bf", align_bytes=64)
         states_by_q = states_raw[:].rearrange("p j q -> p q j")
         nc.vector.tensor_copy(out=states_bf[:, :CAST_SPLIT, :], in_=states_by_q[:, :CAST_SPLIT, :])
         nc.scalar.activation(states_bf[:, CAST_SPLIT:, :], states_by_q[:, CAST_SPLIT:, :], COPY)
@@ -110,12 +113,14 @@ def tile_attend_relayfour_madefour_kernel(
         nc.vector.quantize_mx(
             out=states_c[:].bitcast(FP8X4), scales=states_s[:], in_=states_bf[:].rearrange("p q j -> p (q j)")
         )
+        placed.append(zeroed_window("placed1", "states_bf"))
 
         wq_w_dealt = sb.tile([P, PACK, P], U32, name="wq_w_dealt", align_bytes=64)
-        nc.scalar.copy(
-            out=wq_w_dealt[:].rearrange("p t m -> p m t"),
-            in_=wq_w[:].rearrange("p (m t) -> p m t", t=PACK),
-        )
+        for t in (0, 2):
+            nc.scalar.copy(
+                out=wq_w_dealt[:, t : t + 2, :].rearrange("p t m -> p m t"),
+                in_=wq_w[:].rearrange("p (m t) -> p m t", t=PACK)[:, :, t : t + 2],
+            )
 
         qv = psum.tile([P, PACK, Q], F32, name="qv", tag="bank_qv")
         for t in range(PACK):
@@ -123,13 +128,14 @@ def tile_attend_relayfour_madefour_kernel(
                 out=qv[:, t, :], lhsT=wq_w_dealt[:, t, :].bitcast(FP8X4), lhsT_scale=wq_s_dealt[:, t, :],
                 rhs=states_c[:].bitcast(FP8X4), rhs_scale=states_s[:], start=True, stop=True,
             )
-        qv_bf = sb.tile([P, Q, PACK], BF16, name="qv_bf", align_bytes=64)
+        qv_bf = sb.tile([P, Q, PACK], BF16, name="qv_bf", tag="qv_bf", align_bytes=64)
         nc.scalar.copy(out=qv_bf[:], in_=qv[:].rearrange("p t q -> p q t"))
         qv_c = sb.tile([P, Q], U32, name="qv_c", align_bytes=64)
         qv_s = sb.tile([P, Q], U8, name="qv_s", align_bytes=64)
         nc.vector.quantize_mx(
             out=qv_c[:].bitcast(FP8X4), scales=qv_s[:], in_=qv_bf[:].rearrange("p q t -> p (q t)")
         )
+        placed.append(zeroed_window("placed2", "qv_bf"))
 
         def scores(name, tag, codes, scales, moving, moving_scales):
             bank = psum.tile([P, moving_scales.shape[1]], F32, name=name, tag=tag)

@@ -18,8 +18,9 @@ P = 128
 PACK = 4
 D, K, COLS, SLOTS, Q = 512, 512, 1024, 512, 128
 BANK = 512
-A_PIECE = 256
+A_PIECES = ((0, 256), (256, 512), (512, 768), (768, 896), (896, 1024))
 CAST_SPLIT = 96
+ADD_SPLIT = 704
 HALF = SLOTS // 2
 HALF_COLS = HALF // 16
 
@@ -152,8 +153,7 @@ def tile_attend_relayfour_madefour_kernel(
             return words[:, 2 * c0 : 2 * c1].bitcast(FP4X4)
 
         a = sb.tile([P, COLS], F32, name="a")
-        for piece in range(COLS // A_PIECE):
-            c0, c1 = piece * A_PIECE, (piece + 1) * A_PIECE
+        for piece, (c0, c1) in enumerate(A_PIECES):
             bank = scores("a%d" % piece, "bank%d" % piece, qv_c, qv_s, fp8_cols(keys_w, c0, c1), keys_s[:, c0:c1])
             if piece % 2 == 0:
                 nc.scalar.copy(out=a[:, c0:c1], in_=bank[:])
@@ -161,7 +161,7 @@ def tile_attend_relayfour_madefour_kernel(
                 nc.vector.tensor_copy(out=a[:, c0:c1], in_=bank[:])
 
         halves = [(h * BANK, (h + 1) * BANK) for h in range(COLS // BANK)]
-        b = [scores("b%d" % h, "bank%d" % (4 + h), qv_c, qv_s, fp4_cols(notes_w, c0, c1), notes_s[:, c0:c1])
+        b = [scores("b%d" % h, "bank%d" % (5 + h), qv_c, qv_s, fp4_cols(notes_w, c0, c1), notes_s[:, c0:c1])
              for h, (c0, c1) in enumerate(halves)]
         c = [scores("c%d" % h, "bank%d" % h, states_c, states_s, fp8_cols(users_w, c0, c1), users_s[:, c0:c1])
              for h, (c0, c1) in enumerate(halves)]
@@ -179,8 +179,13 @@ def tile_attend_relayfour_madefour_kernel(
             gather(window, pick, picked[:, :HALF], picked[:, HALF:])
             nc.vector.tensor_copy(placed[stage][:].indirect(put[:]), picked[:])
             window = sb.tile([P, COLS], F32, name="sum%d" % stage)
-            for bank, (c0, c1) in zip(banks, halves):
-                nc.vector.tensor_tensor(window[:, c0:c1], bank[:], placed[stage][:, c0:c1], op)
+            tail = sb.tile([P, COLS - ADD_SPLIT], F32, name="tail%d" % stage)
+            nc.scalar.copy(out=tail[:], in_=banks[1][:, ADD_SPLIT - BANK :])
+            nc.gpsimd.tensor_tensor(window[:, ADD_SPLIT:], tail[:], placed[stage][:, ADD_SPLIT:], op)
+            nc.vector.tensor_tensor(window[:, :BANK], banks[0][:], placed[stage][:, :BANK], op)
+            nc.vector.tensor_tensor(
+                window[:, BANK:ADD_SPLIT], banks[1][:, : ADD_SPLIT - BANK], placed[stage][:, BANK:ADD_SPLIT], op
+            )
 
         y0 = sb.tile([P, HALF], F32, name="y0")
         y1 = sb.tile([P, HALF], F32, name="y1")

@@ -39,7 +39,7 @@ def tile_attend_relayfour_madefour_kernel(
         psum = ctx.enter_context(tc.psum_pool(name="psum", bufs=1))
 
         def zeroed_scales(engine, name, width):
-            tile = sb.tile([P, width], U8, name=name, align_bytes=64)
+            tile = sb.tile([P, width], U8, name=name, tag=name, align_bytes=64)
             engine.memset(tile[:].bitcast(U32), 0)
             return tile
 
@@ -114,7 +114,7 @@ def tile_attend_relayfour_madefour_kernel(
         nc.vector.quantize_mx(
             out=states_c[:].bitcast(FP8X4), scales=states_s[:], in_=states_bf[:].rearrange("p q j -> p (q j)")
         )
-        placed.append(zeroed_window("placed1", "states_bf"))
+        placed.append(zeroed_window("placed1", "wq_s"))
 
         wq_w_dealt = sb.tile([P, PACK, P], U32, name="wq_w_dealt", align_bytes=64)
         for t in (0, 2):

@@ -67,9 +67,9 @@ def tile_attend_relayfour_madefour_kernel(
 
         wq_s = zeroed_scales(nc.vector, "wq_s", K)
         keys_s = zeroed_scales(nc.vector, "keys_s", COLS)
-        notes_s = zeroed_scales(nc.gpsimd, "notes_s", COLS)
-        users_s = zeroed_scales(nc.gpsimd, "users_s", COLS)
-        shelves_s = zeroed_scales(nc.gpsimd, "shelves_s", COLS)
+        notes_s = zeroed_scales(nc.vector, "notes_s", COLS)
+        users_s = zeroed_scales(nc.vector, "users_s", COLS)
+        shelves_s = zeroed_scales(nc.vector, "shelves_s", COLS)
 
         def zeroed_window(name, tag):
             tile = sb.tile([P, COLS], F32, name=name, tag=tag, align_bytes=64)
@@ -81,11 +81,11 @@ def tile_attend_relayfour_madefour_kernel(
         states_raw = sb.tile([P, PACK, Q], F32, name="states_raw")
         nc.sync.dma_start(out=states_raw[:], in_=states.rearrange("(p j) q -> p j q", j=PACK))
         load_scales(nc.sync, wq_s, wq_scales)
-        wq_w = load_fp8("wq_w", wq_words, K)
-        l1 = load_list("l1", offs)
-        l2 = load_list("l2", offs2)
+        wq_w = [load_fp8("wq_w%d" % h, wq_words[:, :, h * (K // 2) : (h + 1) * (K // 2), :], K // 2) for h in range(2)]
         keys_w = load_fp8("keys_w", keys_words, COLS)
         load_scales(nc.sync, keys_s, keys_scales)
+        l1 = load_list("l1", offs)
+        l2 = load_list("l2", offs2)
         notes_w = load_fp4("notes_w", notes_words)
         load_scales(nc.sync, notes_s, notes_scales)
         l3 = load_list("l3", offs3)
@@ -117,10 +117,10 @@ def tile_attend_relayfour_madefour_kernel(
         placed.append(zeroed_window("placed1", "wq_s"))
 
         wq_w_dealt = sb.tile([P, PACK, P], U32, name="wq_w_dealt", align_bytes=64)
-        for t in (0, 2):
+        for h in range(2):
             nc.scalar.copy(
-                out=wq_w_dealt[:, t : t + 2, :].rearrange("p t m -> p m t"),
-                in_=wq_w[:].rearrange("p (m t) -> p m t", t=PACK)[:, :, t : t + 2],
+                out=wq_w_dealt[:, :, h * (P // 2) : (h + 1) * (P // 2)].rearrange("p t m -> p m t"),
+                in_=wq_w[h][:].rearrange("p (m t) -> p m t", t=PACK),
             )
 
         qv = psum.tile([P, PACK, Q], F32, name="qv", tag="bank_qv")

from contextlib import ExitStack

import concourse.mybir as mybir

F32 = mybir.dt.float32
BF16 = mybir.dt.bfloat16
I32 = mybir.dt.int32
U32 = mybir.dt.uint32
U16 = mybir.dt.uint16
U8 = mybir.dt.uint8
FP8X4 = mybir.dt.float8_e4m3fn_x4
FP4X4 = mybir.dt.float4_e2m1fn_x4
ADD = mybir.AluOpType.add
SUBTRACT = mybir.AluOpType.subtract
COPY = mybir.ActivationFunctionType.Copy

P = 128
PACK = 4
D, K, COLS, SLOTS, Q = 512, 512, 1024, 512, 128
BANK = 512
A_PIECES = ((0, 256), (256, 512), (512, 768), (768, 896), (896, 1024))
CAST_SPLIT = 96
ADD_SPLIT = 704
HALF = SLOTS // 2
HALF_COLS = HALF // 16

FLOPS = 2 * D * K * Q + 4 * 2 * K * Q * COLS


def tile_attend_relayfour_madefour_kernel(
    tc, states, wq_words, wq_scales, keys_words, keys_scales, notes_words, notes_scales,
    users_words, users_scales, shelves_words, shelves_scales,
    offs, offs2, offs3, offs4, offs5, offs6, offs7, out,
):
    nc = tc.nc
    with ExitStack() as ctx:
        lists = ctx.enter_context(tc.tile_pool(name="lists", bufs=1))
        sb = ctx.enter_context(tc.tile_pool(name="sb", bufs=1))
        psum = ctx.enter_context(tc.psum_pool(name="psum", bufs=1))

        def zeroed_scales(engine, name, width):
            tile = sb.tile([P, width], U8, name=name, tag=name, align_bytes=64)
            engine.memset(tile[:].bitcast(U32), 0)
            return tile

        def load_scales(queue, tile, rows):
            for quad in range(4):
                queue.dma_start(
                    out=tile[32 * quad : 32 * quad + 4, :].bitcast(I32),
                    in_=rows[0, 4 * quad : 4 * quad + 4, :].bitcast(I32),
                )

        def load_fp8(name, words, width):
            tile = sb.tile([P, width], U32, name=name, align_bytes=64)
            nc.sync.dma_start(out=tile[:].bitcast(I32), in_=words[0].rearrange("p n t -> p (n t)").bitcast(I32))
            return tile

        def load_fp4(name, words):
            tile = sb.tile([P, 2 * COLS], U8, name=name, align_bytes=64)
            nc.sync.dma_start(out=tile[:].bitcast(I32), in_=words[0].bitcast(I32))
            return tile

        def load_list(name, src):
            tile = lists.tile([P, SLOTS // 16], U16, name=name)
            nc.sync.dma_start(tile[:], src)
            return tile

        wq_s = zeroed_scales(nc.vector, "wq_s", K)
        keys_s = zeroed_scales(nc.vector, "keys_s", COLS)
        notes_s = zeroed_scales(nc.vector, "notes_s", COLS)
        users_s = zeroed_scales(nc.vector, "users_s", COLS)
        shelves_s = zeroed_scales(nc.vector, "shelves_s", COLS)

        def zeroed_window(name, tag):
            tile = sb.tile([P, COLS], F32, name=name, tag=tag, align_bytes=64)
            nc.vector.memset(tile[:], 0.0)
            return tile

        placed = [zeroed_window("placed0", "placed0")]

        states_raw = sb.tile([P, PACK, Q], F32, name="states_raw")
        nc.sync.dma_start(out=states_raw[:], in_=states.rearrange("(p j) q -> p j q", j=PACK))
        load_scales(nc.sync, wq_s, wq_scales)
        wq_w = [load_fp8("wq_w%d" % h, wq_words[:, :, h * (K // 2) : (h + 1) * (K // 2), :], K // 2) for h in range(2)]
        keys_w = load_fp8("keys_w", keys_words, COLS)
        load_scales(nc.sync, keys_s, keys_scales)
        l1 = load_list("l1", offs)
        l2 = load_list("l2", offs2)
        notes_w = load_fp4("notes_w", notes_words)
        load_scales(nc.sync, notes_s, notes_scales)
        l3 = load_list("l3", offs3)
        l4 = load_list("l4", offs4)
        users_w = load_fp8("users_w", users_words, COLS)
        load_scales(nc.sync, users_s, users_scales)
        l5 = load_list("l5", offs5)
        l6 = load_list("l6", offs6)
        shelves_w = load_fp4("shelves_w", shelves_words)
        load_scales(nc.sync, shelves_s, shelves_scales)
        l7 = load_list("l7", offs7)

        wq_s_dealt = sb.tile([P, PACK, P], U8, name="wq_s_dealt", align_bytes=64)
        for t in (0, 2):
            nc.vector.tensor_copy(
                out=wq_s_dealt[:, t : t + 2, :].rearrange("p t m -> p m t"),
                in_=wq_s[:].rearrange("p (m t) -> p m t", t=PACK)[:, :, t : t + 2],
            )

        states_bf = sb.tile([P, Q, PACK], BF16, name="states_bf", tag="states_bf", align_bytes=64)
        states_by_q = states_raw[:].rearrange("p j q -> p q j")
        nc.vector.tensor_copy(out=states_bf[:, :CAST_SPLIT, :], in_=states_by_q[:, :CAST_SPLIT, :])
        nc.scalar.activation(states_bf[:, CAST_SPLIT:, :], states_by_q[:, CAST_SPLIT:, :], COPY)
        states_c = sb.tile([P, Q], U32, name="states_c", align_bytes=64)
        states_s = sb.tile([P, Q], U8, name="states_s", align_bytes=64)
        nc.vector.quantize_mx(
            out=states_c[:].bitcast(FP8X4), scales=states_s[:], in_=states_bf[:].rearrange("p q j -> p (q j)")
        )
        placed.append(zeroed_window("placed1", "wq_s"))

        wq_w_dealt = sb.tile([P, PACK, P], U32, name="wq_w_dealt", align_bytes=64)
        for h in range(2):
            nc.scalar.copy(
                out=wq_w_dealt[:, :, h * (P // 2) : (h + 1) * (P // 2)].rearrange("p t m -> p m t"),
                in_=wq_w[h][:].rearrange("p (m t) -> p m t", t=PACK),
            )

        qv = psum.tile([P, PACK, Q], F32, name="qv", tag="bank_qv")
        for t in range(PACK):
            nc.tensor.matmul_mx(
                out=qv[:, t, :], lhsT=wq_w_dealt[:, t, :].bitcast(FP8X4), lhsT_scale=wq_s_dealt[:, t, :],
                rhs=states_c[:].bitcast(FP8X4), rhs_scale=states_s[:], start=True, stop=True,
            )
        qv_bf = sb.tile([P, Q, PACK], BF16, name="qv_bf", tag="qv_bf", align_bytes=64)
        nc.scalar.copy(out=qv_bf[:], in_=qv[:].rearrange("p t q -> p q t"))
        qv_c = sb.tile([P, Q], U32, name="qv_c", align_bytes=64)
        qv_s = sb.tile([P, Q], U8, name="qv_s", align_bytes=64)
        nc.vector.quantize_mx(
            out=qv_c[:].bitcast(FP8X4), scales=qv_s[:], in_=qv_bf[:].rearrange("p q t -> p (q t)")
        )
        placed.append(zeroed_window("placed2", "qv_bf"))

        def scores(name, tag, codes, scales, moving, moving_scales):
            bank = psum.tile([P, moving_scales.shape[1]], F32, name=name, tag=tag)
            nc.tensor.matmul_mx(
                out=bank[:], lhsT=codes[:].bitcast(FP8X4), lhsT_scale=scales[:],
                rhs=moving, rhs_scale=moving_scales, start=True, stop=True,
            )
            return bank

        def fp8_cols(words, c0, c1):
            return words[:, c0:c1].bitcast(FP8X4)

        def fp4_cols(words, c0, c1):
            return words[:, 2 * c0 : 2 * c1].bitcast(FP4X4)

        a = sb.tile([P, COLS], F32, name="a")
        for piece, (c0, c1) in enumerate(A_PIECES):
            bank = scores("a%d" % piece, "bank%d" % piece, qv_c, qv_s, fp8_cols(keys_w, c0, c1), keys_s[:, c0:c1])
            if piece % 2 == 0:
                nc.scalar.copy(out=a[:, c0:c1], in_=bank[:])
            else:
                nc.vector.tensor_copy(out=a[:, c0:c1], in_=bank[:])

        halves = [(h * BANK, (h + 1) * BANK) for h in range(COLS // BANK)]
        b = [scores("b%d" % h, "bank%d" % (5 + h), qv_c, qv_s, fp4_cols(notes_w, c0, c1), notes_s[:, c0:c1])
             for h, (c0, c1) in enumerate(halves)]
        c = [scores("c%d" % h, "bank%d" % h, states_c, states_s, fp8_cols(users_w, c0, c1), users_s[:, c0:c1])
             for h, (c0, c1) in enumerate(halves)]
        d = [scores("d%d" % h, "bank%d" % (2 + h), states_c, states_s, fp4_cols(shelves_w, c0, c1), shelves_s[:, c0:c1])
             for h, (c0, c1) in enumerate(halves)]

        def gather(window, offsets, first, second):
            nc.vector.tensor_copy(first, window[:].indirect(offsets[:, :HALF_COLS]))
            nc.scalar.activation(second, window[:].indirect(offsets[:, HALF_COLS:]), COPY)

        window = a
        stages = ((l1, l2, b, ADD), (l3, l4, c, SUBTRACT), (l5, l6, d, ADD))
        for stage, (pick, put, banks, op) in enumerate(stages):
            picked = sb.tile([P, SLOTS], F32, name="picked%d" % stage)
            gather(window, pick, picked[:, :HALF], picked[:, HALF:])
            nc.vector.tensor_copy(placed[stage][:].indirect(put[:]), picked[:])
            window = sb.tile([P, COLS], F32, name="sum%d" % stage)
            tail = sb.tile([P, COLS - ADD_SPLIT], F32, name="tail%d" % stage)
            nc.scalar.copy(out=tail[:], in_=banks[1][:, ADD_SPLIT - BANK :])
            nc.gpsimd.tensor_tensor(window[:, ADD_SPLIT:], tail[:], placed[stage][:, ADD_SPLIT:], op)
            nc.vector.tensor_tensor(window[:, :BANK], banks[0][:], placed[stage][:, :BANK], op)
            nc.vector.tensor_tensor(
                window[:, BANK:ADD_SPLIT], banks[1][:, : ADD_SPLIT - BANK], placed[stage][:, BANK:ADD_SPLIT], op
            )

        y0 = sb.tile([P, HALF], F32, name="y0")
        y1 = sb.tile([P, HALF], F32, name="y1")
        gather(window, l7, y0[:], y1[:])
        nc.sync.dma_start(out=out[:, :HALF], in_=y0[:])
        nc.scalar.dma_start(out=out[:, HALF:], in_=y1[:])
